import numpy as np
import ml_dtypes


def mxq(x, axis, fmt="e4m3"):
    dtype, down = {"e4m3": (ml_dtypes.float8_e4m3fn, 7), "e5m2": (ml_dtypes.float8_e5m2, 14)}[fmt]
    v = np.moveaxis(np.asarray(x, np.float32).astype(ml_dtypes.bfloat16).astype(np.float64), axis, -1)
    blocks = v.reshape(v.shape[:-1] + (-1, 32))
    amax = np.abs(blocks).max(-1, keepdims=True)
    byte = np.maximum(np.where(amax > 0, np.frexp(amax)[1] - 1 + 127, 0) - down, 1)
    scale = np.exp2(byte - 127.0)
    codes = (blocks / scale).astype(np.float32).astype(dtype).astype(np.float64)
    return np.moveaxis((codes * scale).reshape(v.shape), -1, axis)


WIDE = False


def mx_kscale(k):
    if not WIDE:
        return np.ones(k)
    levels = np.array([10, -10, 5, -5, 0])
    if k % 512:
        return np.exp2(np.random.permutation(np.resize(levels, k // 32))).repeat(32)
    a = np.empty((k // 512, 16))
    for p in range(k // 512):
        a[p, :8] = np.random.permutation(np.resize(levels, 8))
        for g in range(8):
            far = levels[np.abs(levels - a[p, g]) >= 10]
            a[p, g + 8] = far[np.random.randint(len(far))]
    return np.exp2(a.ravel()).repeat(32)


def f64(x):
    return np.asarray(x).astype(np.float64)


def striped(idx):
    return np.tile(idx.reshape(-1, 16).T, (8, 1)).astype(np.uint16)


def unstriped(offs):
    return offs[:16].T.reshape(-1).astype(np.int64)


def pack_weight(w):
    k, n = w.shape
    w = f64(np.asarray(w, np.float32).astype(ml_dtypes.bfloat16)).reshape(k // 32, 32, n)
    amax = np.abs(w).max(1)
    byte = np.clip(np.where(amax > 0, np.frexp(amax)[1] - 1 + 127 - 7, 1), 1, 254)
    scaled = (w * np.exp2(127.0 - byte)[:, None, :]).reshape(k, n).astype(np.float32)
    words = np.ascontiguousarray(scaled.reshape(k // 512, 128, 4, n).transpose(0, 1, 3, 2)).astype(ml_dtypes.float8_e4m3fn).view(np.uint8)
    return words, np.ascontiguousarray(byte.astype(np.uint8).reshape(k // 512, 16, n))


def unpack_weight(words, scales):
    g, p, n, _ = words.shape
    vals = np.ascontiguousarray(words).view(ml_dtypes.float8_e4m3fn).astype(np.float64) * np.repeat(np.exp2(scales.astype(np.float64) - 127.0), 8, axis=1)[..., None]
    return vals.transpose(0, 1, 3, 2).reshape(g * 512, n)


def relu(v):
    return np.maximum(v, 0.0)


K, T, S, V = 512, 2048, 512, 512


def setup_inputs():
    n = np.random.standard_normal
    s = mx_kscale(K)[:, None]
    packed_xT = pack_weight(n((K, T)) * s)
    packed_eT = pack_weight(n((K, T)) * s)
    return {
        "x_words": packed_xT[0],
        "x_scales": packed_xT[1],
        "e_words": packed_eT[0],
        "e_scales": packed_eT[1],
        "hr": (n((K, V)) / np.sqrt(K) / s).astype(np.float32),
        "hi": (n((K, V)) / np.sqrt(K) / s).astype(np.float32),
        "offs": striped(np.random.permutation(T)[:S]),
    }


def reference(x_words, x_scales, e_words, e_scales, hr, hi, offs):
    hrq = mxq(f64(hr), 0, "e4m3")
    xq = unpack_weight(x_words, x_scales)[:, unstriped(offs)]
    hiq = mxq(f64(hi), 0, "e4m3")
    e_offs = unpack_weight(e_words, e_scales)[:, unstriped(offs)]
    z = hiq.T @ e_offs
    re = (hrq.T @ xq) - z
    im = hrq.T @ e_offs + hiq.T @ xq
    pw = (re) ** 2 + (im) ** 2
    near = np.pad(pw, ((0, 0), (2, 0)))[:, :S] + np.pad(pw, ((0, 0), (3, 0)))[:, :S]
    far = np.pad(pw, ((0, 0), (4, 0)))[:, :S] + np.pad(pw, ((0, 0), (5, 0)))[:, :S]
    noise = 0.25 * (near + far) + 0.2
    return relu(pw / noise - 1.0)

@@ -1,0 +1,187 @@
+from contextlib import ExitStack
+
+import concourse.mybir as mybir
+
+K, T, S, V = 512, 2048, 512, 512
+FLOPS = 4 * 2 * K * V * S
+
+F32 = mybir.dt.float32
+BF16 = mybir.dt.bfloat16
+I32 = mybir.dt.int32
+U32 = mybir.dt.uint32
+U16 = mybir.dt.uint16
+U8 = mybir.dt.uint8
+FP8X4 = mybir.dt.float8_e4m3fn_x4
+ALU = mybir.AluOpType
+ACT = mybir.ActivationFunctionType
+
+P = 128
+PACK = 4
+HALF = S // 2
+PAD = 8
+BLOCKS = V // P
+
+
+def tile_picked_ycfar_ca_p_kernel(tc, x_words, x_scales, e_words, e_scales, hr, hi, offs, out):
+    nc = tc.nc
+    with ExitStack() as ctx:
+        keep = ctx.enter_context(tc.tile_pool(name="keep", bufs=1))
+        late = ctx.enter_context(tc.tile_pool(name="late", bufs=1))
+        psum = ctx.enter_context(tc.psum_pool(name="psum", bufs=1))
+
+        offsets = keep.tile([P, S // 16], U16, name="offsets")
+        nc.sync.dma_start(offsets[:], offs)
+
+        def clear_scales(name):
+            window = keep.tile([P, T], U8, name=name, align_bytes=64)
+            nc.vector.memset(window[:].bitcast(I32), 0)
+            return window
+
+        def load_scales(window, scales):
+            for q in range(4):
+                nc.sync.dma_start(window[32 * q : 32 * q + 4, :].bitcast(I32), scales[0, 4 * q : 4 * q + 4, :].bitcast(I32))
+
+        def load_words(words, window, c0, c1):
+            nc.sync.dma_start(window[:, c0:c1].bitcast(I32), words[0].rearrange("p n t -> p (n t)").bitcast(I32)[:, c0:c1])
+
+        def load_filters(h, c0, c1, name, offset):
+            if offset is None:
+                raw = keep.tile([P, PACK, c1 - c0], F32, name=name, align_bytes=64)
+            else:
+                raw = late.tile([P, PACK, c1 - c0], F32, name=name, align_bytes=64, offset=offset)
+            nc.sync.dma_start(raw[:], h.rearrange("(p j) t -> p j t", j=PACK)[:, :, c0:c1])
+            return raw
+
+
+        raw = {}
+
+        def load_pair(b0, b1):
+            for name, h in (("hi", hi), ("hr", hr)):
+                raw[name, b0] = load_filters(h, b0 * P, b1 * P, f"{name}_raw{b0}", None)
+
+        xs_window = clear_scales("xs_window")
+        es_window = clear_scales("es_window")
+        x_window = keep.tile([P, T], U32, name="x_window", align_bytes=64)
+        e_window = keep.tile([P, T], U32, name="e_window", align_bytes=64)
+        load_pair(0, 1)
+        load_words(x_words, x_window, 0, T // 2)
+        load_scales(xs_window, x_scales)
+        load_words(x_words, x_window, T // 2, T)
+        load_scales(es_window, e_scales)
+        load_words(e_words, e_window, 0, T)
+        load_pair(1, 2)
+        load_pair(2, 4)
+        warm = keep.tile([P, 1], F32, name="warm")
+        nc.vector.memset(warm[:], 1.0)
+        warm_out = keep.tile([P, 1], F32, name="warm_out")
+        nc.scalar.activation(warm_out[:], warm[:], ACT.Abs_reciprocal_sqrt)
+
+        power = [keep.tile([P, PAD + S], F32, name=f"power{b}") for b in range(BLOCKS)]
+        near = [keep.tile([P, PAD + S], F32, name=f"near{b}") for b in range(BLOCKS)]
+        for b in range(BLOCKS):
+            nc.vector.memset(power[b][:, 0:PAD], 0.0)
+
+        def gather(window, dtype, c0, c1, name):
+            picked = keep.tile([P, c1 - c0], dtype, name=name, align_bytes=64)
+            nc.vector.tensor_copy(picked[:], window[:].indirect(offsets[:, c0 // 16 : c1 // 16]))
+            return picked
+
+        def interleave(dst, src, on_vector):
+            dst = dst.rearrange("p (c i j) -> p c j i", i=4, j=PACK)
+            view = src.rearrange("p j (c i) -> p c j i", i=4)
+            if on_vector:
+                nc.vector.tensor_copy(dst, view)
+            else:
+                nc.scalar.copy(dst, view)
+
+        def quantize(grouped, width, name):
+            codes = keep.tile([P, width], U32, name=name + "_codes", align_bytes=64)
+            scales = keep.tile([P, width], U8, name=name + "_scales", align_bytes=64)
+            nc.vector.quantize_mx(out=codes[:].bitcast(FP8X4), scales=scales[:], in_=grouped[:])
+            return codes, scales
+
+        filt = {}
+
+        def prepare(b0, b1, r_on_vector, i_on_vector):
+            width = (b1 - b0) * P
+            both = keep.tile([P, 2 * width * PACK], BF16, name=f"both_bf{b0}", align_bytes=64)
+            interleave(both[:, : width * PACK], raw["hi", b0][:], i_on_vector)
+            negated = keep.tile([P, width * PACK], BF16, name=f"hn_bf{b0}", align_bytes=64)
+            nc.vector.tensor_scalar(negated[:], both[:, : width * PACK], -1.0, None, ALU.mult)
+            interleave(both[:, width * PACK :], raw["hr", b0][:], r_on_vector)
+            n_codes, n_scales = quantize(negated, width, f"hn{b0}")
+            codes, scales = quantize(both, 2 * width, f"both{b0}")
+            for b in range(b0, b1):
+                c = (b - b0) * P
+                filt["hn", b] = (n_codes[:, c : c + P], n_scales[:, c : c + P])
+                filt["hi", b] = (codes[:, c : c + P], scales[:, c : c + P])
+                filt["hr", b] = (codes[:, width + c : width + c + P], scales[:, width + c : width + c + P])
+
+        squares = [keep.tile([P, 2, S], F32, name=f"squares{b}") for b in range(BLOCKS)]
+
+        def product(bank_cols, name, b, moving, start):
+            codes, scales = filt[name, b]
+            words, bytes_ = moving
+            nc.tensor.matmul_mx(out=bank_cols, lhsT=codes.bitcast(FP8X4), lhsT_scale=scales,
+                                rhs=words.bitcast(FP8X4), rhs_scale=bytes_, start=start, stop=not start)
+
+        def multiply(b, h):
+            cols = slice(h * HALF, (h + 1) * HALF)
+            x_op = (x_picked[:, cols], xs_picked[:, cols])
+            e_op = (e_picked[h][:], es_picked[:, cols])
+            bank = psum.tile([P, 2, HALF], F32, name=f"bank{b}_{h}")
+            product(bank[:, 0, :], "hr", b, x_op, True)
+            product(bank[:, 0, :], "hn", b, e_op, False)
+            product(bank[:, 1, :], "hr", b, e_op, True)
+            product(bank[:, 1, :], "hi", b, x_op, False)
+            nc.scalar.activation(squares[b][:, :, cols], bank[:], ACT.Square)
+
+        inv = [keep.tile([P, S], F32, name=f"inv{b}") for b in range(BLOCKS)]
+
+        def noise(b, j0, j1):
+            pw, nr = power[b], near[b]
+            nc.vector.tensor_tensor(pw[:, PAD + j0 : PAD + j1], squares[b][:, 0, j0:j1], squares[b][:, 1, j0:j1], ALU.add)
+            lo = j0 - 2 if j0 == 0 else j0
+            nc.vector.tensor_tensor(nr[:, PAD + lo : PAD + j1], pw[:, PAD + lo - 2 : PAD + j1 - 2], pw[:, PAD + lo - 3 : PAD + j1 - 3], ALU.add)
+            total = keep.tile([P, j1 - j0], F32, name=f"total{b}_{j0}")
+            nc.vector.scalar_tensor_tensor(total[:], nr[:, PAD + j0 : PAD + j1], 0.8, nr[:, PAD + j0 - 2 : PAD + j1 - 2], ALU.add, ALU.add)
+            root = keep.tile([P, j1 - j0], F32, name=f"root{b}_{j0}")
+            nc.scalar.activation(root[:], total[:], ACT.Abs_reciprocal_sqrt, scale=0.25)
+            nc.scalar.activation(inv[b][:, j0:j1], root[:], ACT.Square)
+
+        def detect(b, j0, j1, relu_on_vector):
+            ratio = keep.tile([P, j1 - j0], F32, name=f"ratio{b}_{j0}")
+            nc.vector.tensor_tensor(ratio[:], power[b][:, PAD + j0 : PAD + j1], inv[b][:, j0:j1], ALU.mult)
+            result = keep.tile([P, j1 - j0], F32, name=f"result{b}_{j0}")
+            if relu_on_vector:
+                nc.vector.tensor_scalar(result[:], ratio[:], -1.0, 0.0, ALU.add, ALU.max)
+            else:
+                nc.scalar.activation(result[:], ratio[:], ACT.Relu, bias=-1.0)
+            nc.sync.dma_start(out[b * P : (b + 1) * P, j0:j1], result[:])
+
+        prepare(0, 1, False, False)
+        xs_picked = gather(xs_window, U8, 0, S, "xs_picked")
+        x_picked = gather(x_window, U32, 0, S, "x_picked")
+        es_picked = gather(es_window, U8, 0, S, "es_picked")
+        e_picked = [gather(e_window, U32, h * HALF, (h + 1) * HALF, f"e_picked{h}") for h in range(2)]
+        multiply(0, 0)
+        multiply(0, 1)
+        prepare(1, 2, True, False)
+        multiply(1, 0)
+        multiply(1, 1)
+        prepare(2, 4, False, False)
+        multiply(2, 0)
+        multiply(2, 1)
+        multiply(3, 0)
+        multiply(3, 1)
+        noise(0, 0, 256)
+        noise(0, 256, 512)
+        noise(1, 0, 512)
+        noise(2, 0, 512)
+        noise(3, 0, 256)
+        noise(3, 256, 512)
+        detect(0, 0, 512, True)
+        detect(1, 0, 512, True)
+        detect(2, 0, 512, True)
+        detect(3, 0, 256, True)
+        detect(3, 256, 512, True)

@@ -32,14 +32,12 @@ def tile_picked_ycfar_ca_p_kernel(tc, x_words, x_scales, e_words, e_scales, hr, 
         offsets = keep.tile([P, S // 16], U16, name="offsets")
         nc.sync.dma_start(offsets[:], offs)
 
-        def clear_scales(name):
-            window = keep.tile([P, T], U8, name=name, align_bytes=64)
-            nc.vector.memset(window[:].bitcast(I32), 0)
-            return window
-
-        def load_scales(window, scales):
+        def load_scales(scales, name, clear, queue):
+            window = keep.tile([P, T], U8, name=name, tag=name, align_bytes=64)
+            clear.memset(window[:].bitcast(I32), 0)
             for q in range(4):
-                nc.sync.dma_start(window[32 * q : 32 * q + 4, :].bitcast(I32), scales[0, 4 * q : 4 * q + 4, :].bitcast(I32))
+                queue.dma_start(window[32 * q : 32 * q + 4, :].bitcast(I32), scales[0, 4 * q : 4 * q + 4, :].bitcast(I32))
+            return window
 
         def load_words(words, window, c0, c1):
             nc.sync.dma_start(window[:, c0:c1].bitcast(I32), words[0].rearrange("p n t -> p (n t)").bitcast(I32)[:, c0:c1])
@@ -57,17 +55,17 @@ def tile_picked_ycfar_ca_p_kernel(tc, x_words, x_scales, e_words, e_scales, hr, 
 
         def load_pair(b0, b1):
             for name, h in (("hi", hi), ("hr", hr)):
-                raw[name, b0] = load_filters(h, b0 * P, b1 * P, f"{name}_raw{b0}", None)
+                loaded = load_filters(h, b0 * P, b1 * P, f"{name}_raw{b0}", None)
+                for b in range(b0, b1):
+                    raw[name, b] = loaded[:, :, (b - b0) * P : (b - b0 + 1) * P]
 
-        xs_window = clear_scales("xs_window")
-        es_window = clear_scales("es_window")
         x_window = keep.tile([P, T], U32, name="x_window", align_bytes=64)
         e_window = keep.tile([P, T], U32, name="e_window", align_bytes=64)
         load_pair(0, 1)
         load_words(x_words, x_window, 0, T // 2)
-        load_scales(xs_window, x_scales)
+        xs_window = load_scales(x_scales, "xs_window", nc.vector, nc.sync)
         load_words(x_words, x_window, T // 2, T)
-        load_scales(es_window, e_scales)
+        es_window = load_scales(e_scales, "es_window", nc.vector, nc.sync)
         load_words(e_words, e_window, 0, T)
         load_pair(1, 2)
         load_pair(2, 4)
@@ -81,8 +79,8 @@ def tile_picked_ycfar_ca_p_kernel(tc, x_words, x_scales, e_words, e_scales, hr, 
         for b in range(BLOCKS):
             nc.vector.memset(power[b][:, 0:PAD], 0.0)
 
-        def gather(window, dtype, c0, c1, name):
-            picked = keep.tile([P, c1 - c0], dtype, name=name, align_bytes=64)
+        def gather(window, dtype, c0, c1, name, tag):
+            picked = keep.tile([P, c1 - c0], dtype, name=name, tag=tag, align_bytes=64)
             nc.vector.tensor_copy(picked[:], window[:].indirect(offsets[:, c0 // 16 : c1 // 16]))
             return picked
 
@@ -105,10 +103,10 @@ def tile_picked_ycfar_ca_p_kernel(tc, x_words, x_scales, e_words, e_scales, hr, 
         def prepare(b0, b1, r_on_vector, i_on_vector):
             width = (b1 - b0) * P
             both = keep.tile([P, 2 * width * PACK], BF16, name=f"both_bf{b0}", align_bytes=64)
-            interleave(both[:, : width * PACK], raw["hi", b0][:], i_on_vector)
+            interleave(both[:, : width * PACK], raw["hi", b0], i_on_vector)
             negated = keep.tile([P, width * PACK], BF16, name=f"hn_bf{b0}", align_bytes=64)
             nc.vector.tensor_scalar(negated[:], both[:, : width * PACK], -1.0, None, ALU.mult)
-            interleave(both[:, width * PACK :], raw["hr", b0][:], r_on_vector)
+            interleave(both[:, width * PACK :], raw["hr", b0], r_on_vector)
             n_codes, n_scales = quantize(negated, width, f"hn{b0}")
             codes, scales = quantize(both, 2 * width, f"both{b0}")
             for b in range(b0, b1):
@@ -138,50 +136,60 @@ def tile_picked_ycfar_ca_p_kernel(tc, x_words, x_scales, e_words, e_scales, hr, 
 
         inv = [keep.tile([P, S], F32, name=f"inv{b}") for b in range(BLOCKS)]
 
-        def noise(b, j0, j1):
-            pw, nr = power[b], near[b]
-            nc.vector.tensor_tensor(pw[:, PAD + j0 : PAD + j1], squares[b][:, 0, j0:j1], squares[b][:, 1, j0:j1], ALU.add)
-            lo = j0 - 2 if j0 == 0 else j0
-            nc.vector.tensor_tensor(nr[:, PAD + lo : PAD + j1], pw[:, PAD + lo - 2 : PAD + j1 - 2], pw[:, PAD + lo - 3 : PAD + j1 - 3], ALU.add)
-            total = keep.tile([P, j1 - j0], F32, name=f"total{b}_{j0}")
-            nc.vector.scalar_tensor_tensor(total[:], nr[:, PAD + j0 : PAD + j1], 0.8, nr[:, PAD + j0 - 2 : PAD + j1 - 2], ALU.add, ALU.add)
-            root = keep.tile([P, j1 - j0], F32, name=f"root{b}_{j0}")
-            nc.scalar.activation(root[:], total[:], ACT.Abs_reciprocal_sqrt, scale=0.25)
-            nc.scalar.activation(inv[b][:, j0:j1], root[:], ACT.Square)
+        total = [keep.tile([P, S], F32, name=f"total{b}") for b in range(BLOCKS)]
+        root = [keep.tile([P, S], F32, name=f"root{b}") for b in range(BLOCKS)]
 
-        def detect(b, j0, j1, relu_on_vector):
-            ratio = keep.tile([P, j1 - j0], F32, name=f"ratio{b}_{j0}")
-            nc.vector.tensor_tensor(ratio[:], power[b][:, PAD + j0 : PAD + j1], inv[b][:, j0:j1], ALU.mult)
-            result = keep.tile([P, j1 - j0], F32, name=f"result{b}_{j0}")
-            if relu_on_vector:
-                nc.vector.tensor_scalar(result[:], ratio[:], -1.0, 0.0, ALU.add, ALU.max)
-            else:
-                nc.scalar.activation(result[:], ratio[:], ACT.Relu, bias=-1.0)
-            nc.sync.dma_start(out[b * P : (b + 1) * P, j0:j1], result[:])
+        def noise(b, *spans):
+            pw, nr = power[b], near[b]
+            for j0, j1 in spans:
+                nc.vector.tensor_tensor(pw[:, PAD + j0 : PAD + j1], squares[b][:, 0, j0:j1], squares[b][:, 1, j0:j1], ALU.add)
+            for j0, j1 in spans:
+                lo = j0 - 2 if j0 == 0 else j0
+                nc.vector.tensor_tensor(nr[:, PAD + lo : PAD + j1], pw[:, PAD + lo - 2 : PAD + j1 - 2], pw[:, PAD + lo - 3 : PAD + j1 - 3], ALU.add)
+            for j0, j1 in spans:
+                nc.vector.scalar_tensor_tensor(total[b][:, j0:j1], nr[:, PAD + j0 : PAD + j1], 0.8, nr[:, PAD + j0 - 2 : PAD + j1 - 2], ALU.add, ALU.add)
+            for j0, j1 in spans:
+                nc.scalar.activation(root[b][:, j0:j1], total[b][:, j0:j1], ACT.Abs_reciprocal_sqrt, scale=0.25)
+            for j0, j1 in spans:
+                nc.scalar.activation(inv[b][:, j0:j1], root[b][:, j0:j1], ACT.Square)
+
+        ratio = [keep.tile([P, S], F32, name=f"ratio{b}") for b in range(BLOCKS)]
+        result = [keep.tile([P, S], F32, name=f"result{b}") for b in range(BLOCKS)]
+
+        def detect(b, spans, relu_on_vector, stores):
+            for j0, j1 in spans:
+                nc.vector.tensor_tensor(ratio[b][:, j0:j1], power[b][:, PAD + j0 : PAD + j1], inv[b][:, j0:j1], ALU.mult)
+            for j0, j1 in spans:
+                if relu_on_vector:
+                    nc.vector.tensor_scalar(result[b][:, j0:j1], ratio[b][:, j0:j1], -1.0, 0.0, ALU.add, ALU.max)
+                else:
+                    nc.scalar.activation(result[b][:, j0:j1], ratio[b][:, j0:j1], ACT.Relu, bias=-1.0)
+            for j0, j1 in stores:
+                nc.sync.dma_start(out[b * P : (b + 1) * P, j0:j1], result[b][:, j0:j1])
 
         prepare(0, 1, False, False)
-        xs_picked = gather(xs_window, U8, 0, S, "xs_picked")
-        x_picked = gather(x_window, U32, 0, S, "x_picked")
-        es_picked = gather(es_window, U8, 0, S, "es_picked")
-        e_picked = [gather(e_window, U32, h * HALF, (h + 1) * HALF, f"e_picked{h}") for h in range(2)]
+        xs_picked = gather(xs_window, U8, 0, S, "xs_picked", "xs_picked")
+        x_picked = gather(x_window, U32, 0, S, "x_picked", "x_picked")
+        es_picked = gather(es_window, U8, 0, S, "es_picked", "es_picked")
+        e_picked = [gather(e_window, U32, 0, HALF, "e_picked0", "e_picked0"), gather(e_window, U32, HALF, S, "e_picked1", "e_picked1")]
         multiply(0, 0)
         multiply(0, 1)
         prepare(1, 2, True, False)
+        prepare(2, 3, True, False)
+        prepare(3, 4, True, False)
         multiply(1, 0)
         multiply(1, 1)
-        prepare(2, 4, False, False)
         multiply(2, 0)
         multiply(2, 1)
         multiply(3, 0)
         multiply(3, 1)
-        noise(0, 0, 256)
-        noise(0, 256, 512)
-        noise(1, 0, 512)
-        noise(2, 0, 512)
-        noise(3, 0, 256)
-        noise(3, 256, 512)
-        detect(0, 0, 512, True)
-        detect(1, 0, 512, True)
-        detect(2, 0, 512, True)
-        detect(3, 0, 256, True)
-        detect(3, 256, 512, True)
+        whole = [(0, S)]
+        halves = [(0, HALF), (HALF, S)]
+        noise(0, *halves)
+        noise(1, *halves)
+        detect(0, whole, False, whole)
+        noise(2, *halves)
+        detect(1, whole, False, whole)
+        noise(3, *halves)
+        detect(2, halves, True, whole)
+        detect(3, halves, True, halves)

@@ -17,179 +17,179 @@ ACT = mybir.ActivationFunctionType
 
 P = 128
 PACK = 4
-HALF = S // 2
-PAD = 8
 BLOCKS = V // P
+HALF = S // 2
+HALVES = [(0, HALF), (HALF, S)]
+WHOLE = [(0, S)]
+PAD = 8
+ENTRIES_PER_COLUMN = 16
+
+X_FIRST = T // 4
+FIRST_BLOCK_CAST_ON_VECTOR = 2
+FIRST_BLOCK_RELU_ON_VECTOR = 2
 
 
 def tile_picked_ycfar_ca_p_kernel(tc, x_words, x_scales, e_words, e_scales, hr, hi, offs, out):
     nc = tc.nc
     with ExitStack() as ctx:
         keep = ctx.enter_context(tc.tile_pool(name="keep", bufs=1))
-        late = ctx.enter_context(tc.tile_pool(name="late", bufs=1))
         psum = ctx.enter_context(tc.psum_pool(name="psum", bufs=1))
 
-        offsets = keep.tile([P, S // 16], U16, name="offsets")
-        nc.sync.dma_start(offsets[:], offs)
-
-        def load_scales(scales, name, clear, queue):
-            window = keep.tile([P, T], U8, name=name, tag=name, align_bytes=64)
-            clear.memset(window[:].bitcast(I32), 0)
-            for q in range(4):
-                queue.dma_start(window[32 * q : 32 * q + 4, :].bitcast(I32), scales[0, 4 * q : 4 * q + 4, :].bitcast(I32))
-            return window
-
         def load_words(words, window, c0, c1):
-            nc.sync.dma_start(window[:, c0:c1].bitcast(I32), words[0].rearrange("p n t -> p (n t)").bitcast(I32)[:, c0:c1])
+            rows = words[0].rearrange("p n t -> p (n t)").bitcast(I32)
+            nc.sync.dma_start(window[:, c0:c1].bitcast(I32), rows[:, c0:c1])
 
-        def load_filters(h, c0, c1, name, offset):
-            if offset is None:
-                raw = keep.tile([P, PACK, c1 - c0], F32, name=name, align_bytes=64)
-            else:
-                raw = late.tile([P, PACK, c1 - c0], F32, name=name, align_bytes=64, offset=offset)
-            nc.sync.dma_start(raw[:], h.rearrange("(p j) t -> p j t", j=PACK)[:, :, c0:c1])
-            return raw
-
+        def load_scales(scales, name):
+            window = keep.tile([P, T], U8, name=name, align_bytes=64)
+            nc.vector.memset(window[:].bitcast(I32), 0)
+            for q in range(4):
+                rows = scales[0, 4 * q : 4 * q + 4, :]
+                nc.sync.dma_start(window[32 * q : 32 * q + 4, :].bitcast(I32), rows.bitcast(I32))
+            return window
 
         raw = {}
 
-        def load_pair(b0, b1):
+        def load_filters(b0, b1):
             for name, h in (("hi", hi), ("hr", hr)):
-                loaded = load_filters(h, b0 * P, b1 * P, f"{name}_raw{b0}", None)
+                tag = f"{name}_raw{b0}"
+                loaded = keep.tile([P, PACK, (b1 - b0) * P], F32, name=tag, tag=tag, align_bytes=64)
+                nc.sync.dma_start(loaded[:], h.rearrange("(p t) c -> p t c", t=PACK)[:, :, b0 * P : b1 * P])
                 for b in range(b0, b1):
                     raw[name, b] = loaded[:, :, (b - b0) * P : (b - b0 + 1) * P]
 
+        offsets = keep.tile([P, S // ENTRIES_PER_COLUMN], U16, name="offsets")
+        nc.sync.dma_start(offsets[:], offs)
         x_window = keep.tile([P, T], U32, name="x_window", align_bytes=64)
         e_window = keep.tile([P, T], U32, name="e_window", align_bytes=64)
-        load_pair(0, 1)
-        load_words(x_words, x_window, 0, T // 2)
-        xs_window = load_scales(x_scales, "xs_window", nc.vector, nc.sync)
-        load_words(x_words, x_window, T // 2, T)
-        es_window = load_scales(e_scales, "es_window", nc.vector, nc.sync)
+        load_filters(0, 1)
+        load_words(x_words, x_window, 0, X_FIRST)
+        xs_window = load_scales(x_scales, "xs_window")
+        load_words(x_words, x_window, X_FIRST, T)
+        es_window = load_scales(e_scales, "es_window")
         load_words(e_words, e_window, 0, T)
-        load_pair(1, 2)
-        load_pair(2, 4)
-        warm = keep.tile([P, 1], F32, name="warm")
-        nc.vector.memset(warm[:], 1.0)
+        load_filters(1, 2)
+        load_filters(2, BLOCKS)
+
+        warm_in = keep.tile([P, 1], F32, name="warm_in")
+        nc.vector.memset(warm_in[:], 1.0)
         warm_out = keep.tile([P, 1], F32, name="warm_out")
-        nc.scalar.activation(warm_out[:], warm[:], ACT.Abs_reciprocal_sqrt)
+        nc.scalar.activation(warm_out[:], warm_in[:], ACT.Abs_reciprocal_sqrt)
 
         power = [keep.tile([P, PAD + S], F32, name=f"power{b}") for b in range(BLOCKS)]
         near = [keep.tile([P, PAD + S], F32, name=f"near{b}") for b in range(BLOCKS)]
         for b in range(BLOCKS):
             nc.vector.memset(power[b][:, 0:PAD], 0.0)
 
-        def gather(window, dtype, c0, c1, name, tag):
-            picked = keep.tile([P, c1 - c0], dtype, name=name, tag=tag, align_bytes=64)
-            nc.vector.tensor_copy(picked[:], window[:].indirect(offsets[:, c0 // 16 : c1 // 16]))
+        def gather(window, dtype, j0, j1, name):
+            picked = keep.tile([P, j1 - j0], dtype, name=name, align_bytes=64)
+            entries = offsets[:, j0 // ENTRIES_PER_COLUMN : j1 // ENTRIES_PER_COLUMN]
+            nc.vector.tensor_copy(picked[:], window[:].indirect(entries))
             return picked
 
-        def interleave(dst, src, on_vector):
-            dst = dst.rearrange("p (c i j) -> p c j i", i=4, j=PACK)
-            view = src.rearrange("p j (c i) -> p c j i", i=4)
-            if on_vector:
-                nc.vector.tensor_copy(dst, view)
+        def round_and_interleave(dst, name, b):
+            dst = dst.rearrange("p (c i t) -> p c t i", i=4, t=PACK)
+            src = raw[name, b].rearrange("p t (c i) -> p c t i", i=4)
+            if b >= FIRST_BLOCK_CAST_ON_VECTOR:
+                nc.vector.tensor_copy(dst, src)
             else:
-                nc.scalar.copy(dst, view)
+                nc.scalar.copy(dst, src)
 
-        def quantize(grouped, width, name):
-            codes = keep.tile([P, width], U32, name=name + "_codes", align_bytes=64)
-            scales = keep.tile([P, width], U8, name=name + "_scales", align_bytes=64)
-            nc.vector.quantize_mx(out=codes[:].bitcast(FP8X4), scales=scales[:], in_=grouped[:])
+        def quantize(rounded, columns, name):
+            codes = keep.tile([P, columns], U32, name=name + "_codes", align_bytes=64)
+            scales = keep.tile([P, columns], U8, name=name + "_scales", align_bytes=64)
+            nc.vector.quantize_mx(out=codes[:].bitcast(FP8X4), scales=scales[:], in_=rounded[:])
             return codes, scales
 
-        filt = {}
+        filters = {}
 
-        def prepare(b0, b1, r_on_vector, i_on_vector):
-            width = (b1 - b0) * P
-            both = keep.tile([P, 2 * width * PACK], BF16, name=f"both_bf{b0}", align_bytes=64)
-            interleave(both[:, : width * PACK], raw["hi", b0], i_on_vector)
-            negated = keep.tile([P, width * PACK], BF16, name=f"hn_bf{b0}", align_bytes=64)
-            nc.vector.tensor_scalar(negated[:], both[:, : width * PACK], -1.0, None, ALU.mult)
-            interleave(both[:, width * PACK :], raw["hr", b0], r_on_vector)
-            n_codes, n_scales = quantize(negated, width, f"hn{b0}")
-            codes, scales = quantize(both, 2 * width, f"both{b0}")
-            for b in range(b0, b1):
-                c = (b - b0) * P
-                filt["hn", b] = (n_codes[:, c : c + P], n_scales[:, c : c + P])
-                filt["hi", b] = (codes[:, c : c + P], scales[:, c : c + P])
-                filt["hr", b] = (codes[:, width + c : width + c + P], scales[:, width + c : width + c + P])
+        def quantize_block(b):
+            signed = keep.tile([P, 2 * P * PACK], BF16, name=f"hi_bf{b}", align_bytes=64)
+            round_and_interleave(signed[:, : P * PACK], "hi", b)
+            nc.vector.tensor_scalar(signed[:, P * PACK :], signed[:, : P * PACK], -1.0, None, ALU.mult)
+            codes, scales = quantize(signed, 2 * P, f"hi{b}")
+            filters["hi", b] = (codes[:, :P], scales[:, :P])
+            filters["-hi", b] = (codes[:, P:], scales[:, P:])
+            real = keep.tile([P, P * PACK], BF16, name=f"hr_bf{b}", align_bytes=64)
+            round_and_interleave(real[:], "hr", b)
+            codes, scales = quantize(real, P, f"hr{b}")
+            filters["hr", b] = (codes[:], scales[:])
 
-        squares = [keep.tile([P, 2, S], F32, name=f"squares{b}") for b in range(BLOCKS)]
+        def product(acc, stationary, moving, start):
+            nc.tensor.matmul_mx(
+                out=acc,
+                lhsT=stationary[0].bitcast(FP8X4),
+                lhsT_scale=stationary[1],
+                rhs=moving[0].bitcast(FP8X4),
+                rhs_scale=moving[1],
+                start=start,
+                stop=not start,
+            )
 
-        def product(bank_cols, name, b, moving, start):
-            codes, scales = filt[name, b]
-            words, bytes_ = moving
-            nc.tensor.matmul_mx(out=bank_cols, lhsT=codes.bitcast(FP8X4), lhsT_scale=scales,
-                                rhs=words.bitcast(FP8X4), rhs_scale=bytes_, start=start, stop=not start)
+        squares = {}
 
-        def multiply(b, h):
-            cols = slice(h * HALF, (h + 1) * HALF)
-            x_op = (x_picked[:, cols], xs_picked[:, cols])
-            e_op = (e_picked[h][:], es_picked[:, cols])
-            bank = psum.tile([P, 2, HALF], F32, name=f"bank{b}_{h}")
-            product(bank[:, 0, :], "hr", b, x_op, True)
-            product(bank[:, 0, :], "hn", b, e_op, False)
-            product(bank[:, 1, :], "hr", b, e_op, True)
-            product(bank[:, 1, :], "hi", b, x_op, False)
-            nc.scalar.activation(squares[b][:, :, cols], bank[:], ACT.Square)
+        def multiply(b, tag):
+            squares[b] = keep.tile([P, 2, S], F32, name=f"squares{b}", tag=tag, align_bytes=64)
+            for h, (j0, j1) in enumerate(HALVES):
+                x_half = (x_picked[:, j0:j1], xs_picked[:, j0:j1])
+                e_half = (e_picked[h][:], es_picked[:, j0:j1])
+                bank = psum.tile([P, 2, HALF], F32, name=f"bank{b}_{h}")
+                product(bank[:, 0, :], filters["hr", b], x_half, True)
+                product(bank[:, 0, :], filters["-hi", b], e_half, False)
+                product(bank[:, 1, :], filters["hr", b], e_half, True)
+                product(bank[:, 1, :], filters["hi", b], x_half, False)
+                nc.scalar.activation(squares[b][:, :, j0:j1], bank[:], ACT.Square)
 
-        inv = [keep.tile([P, S], F32, name=f"inv{b}") for b in range(BLOCKS)]
-
-        total = [keep.tile([P, S], F32, name=f"total{b}") for b in range(BLOCKS)]
+        inverse = [keep.tile([P, S], F32, name=f"inverse{b}") for b in range(BLOCKS)]
+        noise4 = [keep.tile([P, S], F32, name=f"noise4_{b}") for b in range(BLOCKS)]
         root = [keep.tile([P, S], F32, name=f"root{b}") for b in range(BLOCKS)]
 
-        def noise(b, *spans):
+        def invert_noise(b):
             pw, nr = power[b], near[b]
-            for j0, j1 in spans:
+            for j0, j1 in HALVES:
                 nc.vector.tensor_tensor(pw[:, PAD + j0 : PAD + j1], squares[b][:, 0, j0:j1], squares[b][:, 1, j0:j1], ALU.add)
-            for j0, j1 in spans:
-                lo = j0 - 2 if j0 == 0 else j0
-                nc.vector.tensor_tensor(nr[:, PAD + lo : PAD + j1], pw[:, PAD + lo - 2 : PAD + j1 - 2], pw[:, PAD + lo - 3 : PAD + j1 - 3], ALU.add)
-            for j0, j1 in spans:
-                nc.vector.scalar_tensor_tensor(total[b][:, j0:j1], nr[:, PAD + j0 : PAD + j1], 0.8, nr[:, PAD + j0 - 2 : PAD + j1 - 2], ALU.add, ALU.add)
-            for j0, j1 in spans:
-                nc.scalar.activation(root[b][:, j0:j1], total[b][:, j0:j1], ACT.Abs_reciprocal_sqrt, scale=0.25)
-            for j0, j1 in spans:
-                nc.scalar.activation(inv[b][:, j0:j1], root[b][:, j0:j1], ACT.Square)
+            for j0, j1 in HALVES:
+                lo = -2 if j0 == 0 else j0
+                two_back, three_back = pw[:, PAD + lo - 2 : PAD + j1 - 2], pw[:, PAD + lo - 3 : PAD + j1 - 3]
+                nc.vector.tensor_tensor(nr[:, PAD + lo : PAD + j1], two_back, three_back, ALU.add)
+            for j0, j1 in HALVES:
+                far = nr[:, PAD + j0 - 2 : PAD + j1 - 2]
+                nc.vector.scalar_tensor_tensor(noise4[b][:, j0:j1], nr[:, PAD + j0 : PAD + j1], 0.8, far, ALU.add, ALU.add)
+            for j0, j1 in HALVES:
+                nc.scalar.activation(root[b][:, j0:j1], noise4[b][:, j0:j1], ACT.Abs_reciprocal_sqrt, scale=0.25)
+            for j0, j1 in HALVES:
+                nc.scalar.activation(inverse[b][:, j0:j1], root[b][:, j0:j1], ACT.Square)
 
         ratio = [keep.tile([P, S], F32, name=f"ratio{b}") for b in range(BLOCKS)]
         result = [keep.tile([P, S], F32, name=f"result{b}") for b in range(BLOCKS)]
 
-        def detect(b, spans, relu_on_vector, stores):
+        def detect(b):
+            relu_on_vector = b >= FIRST_BLOCK_RELU_ON_VECTOR
+            spans = HALVES if relu_on_vector else WHOLE
             for j0, j1 in spans:
-                nc.vector.tensor_tensor(ratio[b][:, j0:j1], power[b][:, PAD + j0 : PAD + j1], inv[b][:, j0:j1], ALU.mult)
+                nc.vector.tensor_tensor(ratio[b][:, j0:j1], power[b][:, PAD + j0 : PAD + j1], inverse[b][:, j0:j1], ALU.mult)
             for j0, j1 in spans:
                 if relu_on_vector:
                     nc.vector.tensor_scalar(result[b][:, j0:j1], ratio[b][:, j0:j1], -1.0, 0.0, ALU.add, ALU.max)
                 else:
                     nc.scalar.activation(result[b][:, j0:j1], ratio[b][:, j0:j1], ACT.Relu, bias=-1.0)
-            for j0, j1 in stores:
+            for j0, j1 in HALVES if b == BLOCKS - 1 else WHOLE:
                 nc.sync.dma_start(out[b * P : (b + 1) * P, j0:j1], result[b][:, j0:j1])
 
-        prepare(0, 1, False, False)
-        xs_picked = gather(xs_window, U8, 0, S, "xs_picked", "xs_picked")
-        x_picked = gather(x_window, U32, 0, S, "x_picked", "x_picked")
-        es_picked = gather(es_window, U8, 0, S, "es_picked", "es_picked")
-        e_picked = [gather(e_window, U32, 0, HALF, "e_picked0", "e_picked0"), gather(e_window, U32, HALF, S, "e_picked1", "e_picked1")]
-        multiply(0, 0)
-        multiply(0, 1)
-        prepare(1, 2, True, False)
-        prepare(2, 3, True, False)
-        prepare(3, 4, True, False)
-        multiply(1, 0)
-        multiply(1, 1)
-        multiply(2, 0)
-        multiply(2, 1)
-        multiply(3, 0)
-        multiply(3, 1)
-        whole = [(0, S)]
-        halves = [(0, HALF), (HALF, S)]
-        noise(0, *halves)
-        noise(1, *halves)
-        detect(0, whole, False, whole)
-        noise(2, *halves)
-        detect(1, whole, False, whole)
-        noise(3, *halves)
-        detect(2, halves, True, whole)
-        detect(3, halves, True, halves)
+        quantize_block(0)
+        xs_picked = gather(xs_window, U8, 0, S, "xs_picked")
+        x_picked = gather(x_window, U32, 0, S, "x_picked")
+        es_picked = gather(es_window, U8, 0, S, "es_picked")
+        e_picked = [gather(e_window, U32, j0, j1, f"e_picked{j0}") for j0, j1 in HALVES]
+        last_cast_on_scalar = FIRST_BLOCK_CAST_ON_VECTOR - 1
+        for b in range(1, FIRST_BLOCK_CAST_ON_VECTOR):
+            quantize_block(b)
+        multiply(0, f"hr_raw{last_cast_on_scalar}")
+        for b in range(FIRST_BLOCK_CAST_ON_VECTOR, BLOCKS):
+            quantize_block(b)
+        for b in range(1, BLOCKS):
+            multiply(b, f"squares{b}")
+        for b in range(BLOCKS):
+            invert_noise(b)
+            if b >= 1:
+                detect(b - 1)
+        detect(BLOCKS - 1)

from contextlib import ExitStack

import concourse.mybir as mybir

K, T, S, V = 512, 2048, 512, 512
FLOPS = 4 * 2 * K * V * S

F32 = mybir.dt.float32
BF16 = mybir.dt.bfloat16
I32 = mybir.dt.int32
U32 = mybir.dt.uint32
U16 = mybir.dt.uint16
U8 = mybir.dt.uint8
FP8X4 = mybir.dt.float8_e4m3fn_x4
ALU = mybir.AluOpType
ACT = mybir.ActivationFunctionType

P = 128
PACK = 4
BLOCKS = V // P
HALF = S // 2
HALVES = [(0, HALF), (HALF, S)]
WHOLE = [(0, S)]
PAD = 8
ENTRIES_PER_COLUMN = 16

X_FIRST = T // 4
FIRST_BLOCK_CAST_ON_VECTOR = 2
FIRST_BLOCK_RELU_ON_VECTOR = 2


def tile_picked_ycfar_ca_p_kernel(tc, x_words, x_scales, e_words, e_scales, hr, hi, offs, out):
    nc = tc.nc
    with ExitStack() as ctx:
        keep = ctx.enter_context(tc.tile_pool(name="keep", bufs=1))
        psum = ctx.enter_context(tc.psum_pool(name="psum", bufs=1))

        def load_words(words, window, c0, c1):
            rows = words[0].rearrange("p n t -> p (n t)").bitcast(I32)
            nc.sync.dma_start(window[:, c0:c1].bitcast(I32), rows[:, c0:c1])

        def load_scales(scales, name):
            window = keep.tile([P, T], U8, name=name, align_bytes=64)
            nc.vector.memset(window[:].bitcast(I32), 0)
            for q in range(4):
                rows = scales[0, 4 * q : 4 * q + 4, :]
                nc.sync.dma_start(window[32 * q : 32 * q + 4, :].bitcast(I32), rows.bitcast(I32))
            return window

        raw = {}

        def load_filters(b0, b1):
            for name, h in (("hi", hi), ("hr", hr)):
                tag = f"{name}_raw{b0}"
                loaded = keep.tile([P, PACK, (b1 - b0) * P], F32, name=tag, tag=tag, align_bytes=64)
                nc.sync.dma_start(loaded[:], h.rearrange("(p t) c -> p t c", t=PACK)[:, :, b0 * P : b1 * P])
                for b in range(b0, b1):
                    raw[name, b] = loaded[:, :, (b - b0) * P : (b - b0 + 1) * P]

        offsets = keep.tile([P, S // ENTRIES_PER_COLUMN], U16, name="offsets")
        nc.sync.dma_start(offsets[:], offs)
        x_window = keep.tile([P, T], U32, name="x_window", align_bytes=64)
        e_window = keep.tile([P, T], U32, name="e_window", align_bytes=64)
        load_filters(0, 1)
        load_words(x_words, x_window, 0, X_FIRST)
        xs_window = load_scales(x_scales, "xs_window")
        load_words(x_words, x_window, X_FIRST, T)
        es_window = load_scales(e_scales, "es_window")
        load_words(e_words, e_window, 0, T)
        load_filters(1, 2)
        load_filters(2, BLOCKS)

        warm_in = keep.tile([P, 1], F32, name="warm_in")
        nc.vector.memset(warm_in[:], 1.0)
        warm_out = keep.tile([P, 1], F32, name="warm_out")
        nc.scalar.activation(warm_out[:], warm_in[:], ACT.Abs_reciprocal_sqrt)

        power = [keep.tile([P, PAD + S], F32, name=f"power{b}") for b in range(BLOCKS)]
        near = [keep.tile([P, PAD + S], F32, name=f"near{b}") for b in range(BLOCKS)]
        for b in range(BLOCKS):
            nc.vector.memset(power[b][:, 0:PAD], 0.0)

        def gather(window, dtype, j0, j1, name):
            picked = keep.tile([P, j1 - j0], dtype, name=name, align_bytes=64)
            entries = offsets[:, j0 // ENTRIES_PER_COLUMN : j1 // ENTRIES_PER_COLUMN]
            nc.vector.tensor_copy(picked[:], window[:].indirect(entries))
            return picked

        def round_and_interleave(dst, name, b):
            dst = dst.rearrange("p (c i t) -> p c t i", i=4, t=PACK)
            src = raw[name, b].rearrange("p t (c i) -> p c t i", i=4)
            if b >= FIRST_BLOCK_CAST_ON_VECTOR:
                nc.vector.tensor_copy(dst, src)
            else:
                nc.scalar.copy(dst, src)

        def quantize(rounded, columns, name):
            codes = keep.tile([P, columns], U32, name=name + "_codes", align_bytes=64)
            scales = keep.tile([P, columns], U8, name=name + "_scales", align_bytes=64)
            nc.vector.quantize_mx(out=codes[:].bitcast(FP8X4), scales=scales[:], in_=rounded[:])
            return codes, scales

        filters = {}

        def quantize_block(b):
            signed = keep.tile([P, 2 * P * PACK], BF16, name=f"hi_bf{b}", align_bytes=64)
            round_and_interleave(signed[:, : P * PACK], "hi", b)
            nc.vector.tensor_scalar(signed[:, P * PACK :], signed[:, : P * PACK], -1.0, None, ALU.mult)
            codes, scales = quantize(signed, 2 * P, f"hi{b}")
            filters["hi", b] = (codes[:, :P], scales[:, :P])
            filters["-hi", b] = (codes[:, P:], scales[:, P:])
            real = keep.tile([P, P * PACK], BF16, name=f"hr_bf{b}", align_bytes=64)
            round_and_interleave(real[:], "hr", b)
            codes, scales = quantize(real, P, f"hr{b}")
            filters["hr", b] = (codes[:], scales[:])

        def product(acc, stationary, moving, start):
            nc.tensor.matmul_mx(
                out=acc,
                lhsT=stationary[0].bitcast(FP8X4),
                lhsT_scale=stationary[1],
                rhs=moving[0].bitcast(FP8X4),
                rhs_scale=moving[1],
                start=start,
                stop=not start,
            )

        squares = {}

        def multiply(b, tag):
            squares[b] = keep.tile([P, 2, S], F32, name=f"squares{b}", tag=tag, align_bytes=64)
            for h, (j0, j1) in enumerate(HALVES):
                x_half = (x_picked[:, j0:j1], xs_picked[:, j0:j1])
                e_half = (e_picked[h][:], es_picked[:, j0:j1])
                bank = psum.tile([P, 2, HALF], F32, name=f"bank{b}_{h}")
                product(bank[:, 0, :], filters["hr", b], x_half, True)
                product(bank[:, 0, :], filters["-hi", b], e_half, False)
                product(bank[:, 1, :], filters["hr", b], e_half, True)
                product(bank[:, 1, :], filters["hi", b], x_half, False)
                nc.scalar.activation(squares[b][:, :, j0:j1], bank[:], ACT.Square)

        inverse = [keep.tile([P, S], F32, name=f"inverse{b}") for b in range(BLOCKS)]
        noise4 = [keep.tile([P, S], F32, name=f"noise4_{b}") for b in range(BLOCKS)]
        root = [keep.tile([P, S], F32, name=f"root{b}") for b in range(BLOCKS)]

        def invert_noise(b):
            pw, nr = power[b], near[b]
            for j0, j1 in HALVES:
                nc.vector.tensor_tensor(pw[:, PAD + j0 : PAD + j1], squares[b][:, 0, j0:j1], squares[b][:, 1, j0:j1], ALU.add)
            for j0, j1 in HALVES:
                lo = -2 if j0 == 0 else j0
                two_back, three_back = pw[:, PAD + lo - 2 : PAD + j1 - 2], pw[:, PAD + lo - 3 : PAD + j1 - 3]
                nc.vector.tensor_tensor(nr[:, PAD + lo : PAD + j1], two_back, three_back, ALU.add)
            for j0, j1 in HALVES:
                far = nr[:, PAD + j0 - 2 : PAD + j1 - 2]
                nc.vector.scalar_tensor_tensor(noise4[b][:, j0:j1], nr[:, PAD + j0 : PAD + j1], 0.8, far, ALU.add, ALU.add)
            for j0, j1 in HALVES:
                nc.scalar.activation(root[b][:, j0:j1], noise4[b][:, j0:j1], ACT.Abs_reciprocal_sqrt, scale=0.25)
            for j0, j1 in HALVES:
                nc.scalar.activation(inverse[b][:, j0:j1], root[b][:, j0:j1], ACT.Square)

        ratio = [keep.tile([P, S], F32, name=f"ratio{b}") for b in range(BLOCKS)]
        result = [keep.tile([P, S], F32, name=f"result{b}") for b in range(BLOCKS)]

        def detect(b):
            relu_on_vector = b >= FIRST_BLOCK_RELU_ON_VECTOR
            spans = HALVES if relu_on_vector else WHOLE
            for j0, j1 in spans:
                nc.vector.tensor_tensor(ratio[b][:, j0:j1], power[b][:, PAD + j0 : PAD + j1], inverse[b][:, j0:j1], ALU.mult)
            for j0, j1 in spans:
                if relu_on_vector:
                    nc.vector.tensor_scalar(result[b][:, j0:j1], ratio[b][:, j0:j1], -1.0, 0.0, ALU.add, ALU.max)
                else:
                    nc.scalar.activation(result[b][:, j0:j1], ratio[b][:, j0:j1], ACT.Relu, bias=-1.0)
            for j0, j1 in HALVES if b == BLOCKS - 1 else WHOLE:
                nc.sync.dma_start(out[b * P : (b + 1) * P, j0:j1], result[b][:, j0:j1])

        quantize_block(0)
        xs_picked = gather(xs_window, U8, 0, S, "xs_picked")
        x_picked = gather(x_window, U32, 0, S, "x_picked")
        es_picked = gather(es_window, U8, 0, S, "es_picked")
        e_picked = [gather(e_window, U32, j0, j1, f"e_picked{j0}") for j0, j1 in HALVES]
        last_cast_on_scalar = FIRST_BLOCK_CAST_ON_VECTOR - 1
        for b in range(1, FIRST_BLOCK_CAST_ON_VECTOR):
            quantize_block(b)
        multiply(0, f"hr_raw{last_cast_on_scalar}")
        for b in range(FIRST_BLOCK_CAST_ON_VECTOR, BLOCKS):
            quantize_block(b)
        for b in range(1, BLOCKS):
            multiply(b, f"squares{b}")
        for b in range(BLOCKS):
            invert_noise(b)
            if b >= 1:
                detect(b - 1)
        detect(BLOCKS - 1)
